import numpy as np
import ml_dtypes


def mxq(x, axis, fmt="e4m3"):
    dtype, down = {"e4m3": (ml_dtypes.float8_e4m3fn, 7), "e5m2": (ml_dtypes.float8_e5m2, 14)}[fmt]
    v = np.moveaxis(np.asarray(x, np.float32).astype(ml_dtypes.bfloat16).astype(np.float64), axis, -1)
    blocks = v.reshape(v.shape[:-1] + (-1, 32))
    amax = np.abs(blocks).max(-1, keepdims=True)
    byte = np.maximum(np.where(amax > 0, np.frexp(amax)[1] - 1 + 127, 0) - down, 1)
    scale = np.exp2(byte - 127.0)
    codes = (blocks / scale).astype(np.float32).astype(dtype).astype(np.float64)
    return np.moveaxis((codes * scale).reshape(v.shape), -1, axis)


WIDE = False


def mx_kscale(k):
    if not WIDE:
        return np.ones(k)
    levels = np.array([10, -10, 5, -5, 0])
    if k % 512:
        return np.exp2(np.random.permutation(np.resize(levels, k // 32))).repeat(32)
    a = np.empty((k // 512, 16))
    for p in range(k // 512):
        a[p, :8] = np.random.permutation(np.resize(levels, 8))
        for g in range(8):
            far = levels[np.abs(levels - a[p, g]) >= 10]
            a[p, g + 8] = far[np.random.randint(len(far))]
    return np.exp2(a.ravel()).repeat(32)


def f64(x):
    return np.asarray(x).astype(np.float64)


def striped(idx):
    return np.tile(np.asarray(idx).reshape(-1, 16).T, (8, 1)).astype(np.uint16)


def unstriped(offs):
    return offs[:16].T.reshape(-1).astype(np.int64)


E2M1 = np.array([0.0, 0.5, 1.0, 1.5, 2.0, 3.0, 4.0, 6.0, -0.0, -0.5, -1.0, -1.5, -2.0, -3.0, -4.0, -6.0])


def pack_weight(w, fmt):
    k, n = w.shape
    w = f64(np.asarray(w, np.float32).astype(ml_dtypes.bfloat16)).reshape(k // 32, 32, n)
    amax = np.abs(w).max(1)
    if fmt == "e4m3":
        byte = np.frexp(amax)[1] - 1 + 127 - 7
    else:
        mant, ex = np.frexp(amax / 6.0)
        byte = np.where(mant > 0.5, ex, ex - 1) + 127
    byte = np.clip(np.where(amax > 0, byte, 1), 1, 254)
    scaled = (w * np.exp2(127.0 - byte)[:, None, :]).reshape(k, n).astype(np.float32)
    by_word = np.ascontiguousarray(scaled.reshape(k // 512, 128, 4, n).transpose(0, 1, 3, 2))
    if fmt == "e4m3":
        words = by_word.astype(ml_dtypes.float8_e4m3fn).view(np.uint8)
    else:
        c = by_word.astype(ml_dtypes.float4_e2m1fn).view(np.uint8) & 0xF
        words = (c[..., 0::2] | (c[..., 1::2] << 4)).reshape(k // 512, 128, 2 * n)
    return np.ascontiguousarray(words), np.ascontiguousarray(byte.astype(np.uint8).reshape(k // 512, 16, n))


def unpack_weight(words, scales, fmt):
    g, _, n = scales.shape
    words = np.ascontiguousarray(words).reshape(g, 128, n, -1)
    if fmt == "e4m3":
        vals = words.view(ml_dtypes.float8_e4m3fn).astype(np.float64)
    else:
        nib = np.empty((g, 128, n, 4), np.uint8)
        nib[..., 0::2] = words & 0xF
        nib[..., 1::2] = words >> 4
        vals = E2M1[nib]
    vals = vals * np.repeat(np.exp2(scales.astype(np.float64) - 127.0), 8, axis=1)[..., None]
    return vals.transpose(0, 1, 3, 2).reshape(g * 512, n)


def bf(x):
    return np.asarray(x, np.float32).astype(ml_dtypes.bfloat16)


def planes(Y):
    r, m = Y.shape
    b = f64(bf(Y)).reshape(r // 32, 32, m)
    amax = np.abs(b).max(1)
    byte = np.clip(np.where(amax > 0, np.frexp(amax)[1] - 1 + 127 - 7, 1), 1, 254)
    codes = (b * np.exp2(127.0 - byte)[:, None, :]).reshape(r, m).astype(np.float32).astype(ml_dtypes.float8_e4m3fn).view(np.uint8)
    words = codes.reshape(r // 512, 128, 4, m).transpose(0, 1, 3, 2)
    return np.ascontiguousarray(words), np.ascontiguousarray(byte.astype(np.uint8).reshape(r // 512, 16, m))


D, E, T, I, Q, G = 512, 512, 1024, 256, 512, 16


def setup_inputs():
    n = np.random.standard_normal
    idx = np.random.permutation(T)[:I]
    fd = mx_kscale(D)
    fq = mx_kscale(Q)
    keysp = pack_weight(n((D, T)) / fd[:, None], "e4m3")
    return {
        "query": (n((D, Q)) * 0.5 / np.sqrt(D) * fd[:, None]).astype(np.float32),
        "qs": (np.random.uniform(8.0, 32.0, (Q, 1)) * fq[:, None]).astype(np.float32),
        "grows": (n((Q, E)) / fq[:, None]).astype(np.float32),
        "vals": (n((E, T))).astype(np.float32),
        "keys_words": keysp[0],
        "keys_scales": keysp[1],
        "gain": (np.random.uniform(0.5, 2.0, (E, 1))).astype(np.float32),
        "pre": (np.random.uniform(0.3, 2.5, (1, I))).astype(np.float32),
        "sg": (np.random.uniform(0.5, 2.0, (1, I))).astype(np.float32),
        "old": (0.5 * n((E, I))).astype(np.float32),
        "offs": striped(idx),
    }


def reference(query, qs, grows, vals, keys_words, keys_scales, gain, pre, sg, old, offs):
    idx = unstriped(offs)
    keysu = unpack_weight(keys_words, keys_scales, "e4m3")
    queryq = mxq(f64(query), 0, "e4m3")
    keysidxg = keysu[:, idx]
    a = queryq.T @ keysidxg
    p = np.exp(a - np.max(a, axis=1, keepdims=True))
    w = p * f64(qs) / np.sum(p, axis=1, keepdims=True)
    growsq = mxq(f64(grows), 0, "e4m3")
    wq = mxq(w, 0, "e4m3")
    c0 = growsq.T @ wq
    x1 = f64(vals)[:, idx] * f64(pre)
    m1 = np.sqrt(np.square(x1).reshape(E, G, I // G).mean(axis=2) + 0.05)
    mr = np.repeat(m1, I // G, axis=1)
    dmr = c0 * f64(gain) * x1 / np.square(mr) * (-1.0)
    dm1 = dmr.reshape(E, G, I // G).sum(axis=2)
    e1 = dm1 * 0.5 / np.sqrt(np.square(x1).reshape(E, G, I // G).mean(axis=2) + 0.05) / 16.0
    r1 = np.repeat(e1, I // G, axis=1)
    dx1 = c0 * f64(gain) / mr + r1 * x1 * 2.0
    y = dx1 * f64(sg) + f64(old)
    words, scales = planes(y)
    return y, words, scales

@@ -1,0 +1,359 @@
+from contextlib import ExitStack
+
+import concourse.mybir as mybir
+from concourse.masks import make_identity
+
+D, E, T, I, Q, G = 512, 512, 1024, 256, 512, 16
+PAGE = I // G
+P = 128
+PACK = 4
+FLOPS = 2 * D * Q * I + 2 * Q * E * I
+
+F32 = mybir.dt.float32
+BF16 = mybir.dt.bfloat16
+I32 = mybir.dt.int32
+U32 = mybir.dt.uint32
+U16 = mybir.dt.uint16
+U8 = mybir.dt.uint8
+FP8X4 = mybir.dt.float8_e4m3fn_x4
+ALU = mybir.AluOpType
+ACT = mybir.ActivationFunctionType
+AX = mybir.AxisListType
+
+
+def tile_attend_bvpagescaled_d_pl_kernel(
+    tc, query, qs, grows, vals, keys_words, keys_scales, gain, pre, sg, old, offs, out_0, out_1, out_2
+):
+    nc = tc.nc
+    with ExitStack() as ctx:
+        sb = ctx.enter_context(tc.tile_pool(name="sb", bufs=1))
+        ps = ctx.enter_context(tc.psum_pool(name="ps", bufs=1))
+
+        offsets = sb.tile([P, I // 16], U16, name="offsets")
+        kw = sb.tile([P, T], U32, name="kw")
+        ks = sb.tile([P, T], U8, name="ks")
+        q_raw = [sb.tile([P, PACK, Q // 2], F32, name=f"q_raw{h}") for h in range(2)]
+        g_raw = sb.tile([P, PACK, E], F32, name="g_raw", tag="graw")
+        v_raw = [sb.tile([P, T], F32, name=f"v_raw{t}") for t in range(PACK)]
+        old_sb = sb.tile([P, PACK, I], F32, name="old_sb")
+        pre_col = sb.tile([P, 2], F32, name="pre_col")
+        sg_col = sb.tile([P, 2], F32, name="sg_col")
+        qs_col = sb.tile([P, PACK], F32, name="qs_col")
+        gain_col = sb.tile([P, PACK], F32, name="gain_col")
+        ident = sb.tile([P, P], F32, name="ident")
+
+        v_rows = vals.rearrange("(p t) c -> p t c", t=PACK)
+
+        def load_kw():
+            nc.sync.dma_start(out=kw[:].bitcast(I32), in_=keys_words[0].rearrange("p c r -> p (c r)").bitcast(I32))
+
+        def load_q(h):
+            cols = slice(h * Q // 2, (h + 1) * Q // 2)
+            nc.sync.dma_start(out=q_raw[h][:], in_=query.rearrange("(p j) q -> p j q", j=PACK)[:, :, cols])
+
+        def load_g():
+            nc.sync.dma_start(out=g_raw[:], in_=grows.rearrange("(p j) e -> p j e", j=PACK))
+
+        def load_v(t):
+            nc.sync.dma_start(out=v_raw[t][:], in_=v_rows[:, t, :])
+
+        def load_old():
+            nc.sync.dma_start(out=old_sb[:], in_=old.rearrange("(p t) i -> p t i", t=PACK))
+
+        def load_ks():
+            for quad in range(4):
+                nc.sync.dma_start(
+                    out=ks[32 * quad : 32 * quad + 4, :].bitcast(I32),
+                    in_=keys_scales[0, 4 * quad : 4 * quad + 4, :].bitcast(I32),
+                )
+
+        def load_pre():
+            nc.sync.dma_start(out=pre_col[:], in_=pre.rearrange("o (p h) -> p (o h)", h=2))
+
+        def load_sg():
+            nc.sync.dma_start(out=sg_col[:], in_=sg.rearrange("o (p h) -> p (o h)", h=2))
+
+        def load_qs():
+            nc.sync.dma_start(out=qs_col[:], in_=qs.rearrange("(p t) o -> p (t o)", t=PACK))
+
+        def load_gain():
+            nc.sync.dma_start(out=gain_col[:], in_=gain.rearrange("(p t) o -> p (t o)", t=PACK))
+
+        nc.gpsimd.memset(ks[:].bitcast(I32), 0)
+        nc.sync.dma_start(offsets[:], offs)
+        load_ks()
+        load_pre()
+        load_q(0)
+        load_kw()
+        load_q(1)
+        load_qs()
+        load_v(0)
+        load_g()
+        load_sg()
+        load_gain()
+        load_v(1)
+        load_v(2)
+        load_v(3)
+        load_old()
+        make_identity(nc, ident[:])
+
+        rows = sb.tile([P, 2, I], F32, name="rows")
+        pre_row = rows[:, 0, :]
+        sg_row = rows[:, 1, :]
+
+        def spread_row(v, col):
+            spread = ps.tile([P, 2, P], F32, name=f"spread{v}")
+            for h in range(2):
+                nc.tensor.transpose(spread[:, h, :], col[:, h : h + 1].to_broadcast([P, P]), ident[:])
+            nc.scalar.activation(
+                out=rows[:, v, :].rearrange("p (i h) -> p i h", h=2),
+                in_=spread[:].rearrange("p h i -> p i h"),
+                func=ACT.Copy,
+            )
+
+        def deal(engine, dst, src, lo, hi, base=0):
+            out = dst[:, :, lo:hi, :].rearrange("p t m j -> p m j t")
+            in_ = src[:, :, PACK * (lo - base) : PACK * (hi - base)].rearrange("p j (m t) -> p m j t", t=PACK)
+            if engine == "v":
+                nc.vector.tensor_copy(out=out, in_=in_)
+            elif engine == "g":
+                nc.gpsimd.tensor_scalar(out=out, in0=in_, scalar1=1.0, scalar2=0.0, op0=ALU.mult, op1=ALU.add)
+            else:
+                nc.scalar.copy(out=out, in_=in_)
+
+        def quantize(codes, scales, src):
+            nc.vector.quantize_mx(out=codes.bitcast(FP8X4), scales=scales, in_=src)
+
+        kg = sb.tile([P, I], U32, name="kg", align_bytes=64)
+        ksg = sb.tile([P, I], U8, name="ksg", align_bytes=64)
+        qb = sb.tile([P, PACK, P, PACK], BF16, name="qb", align_bytes=64)
+        qc = sb.tile([P, Q], U32, name="qc", align_bytes=64)
+        qsc = sb.tile([P, Q], U8, name="qsc", align_bytes=64)
+        gb = sb.tile([P, PACK, P, PACK], BF16, name="gb", align_bytes=64)
+        gc = sb.tile([P, E], U32, name="gc", align_bytes=64)
+        gsc = sb.tile([P, E], U8, name="gsc", align_bytes=64)
+        wb = sb.tile([P, I, PACK], BF16, name="wb", align_bytes=64)
+        wc = sb.tile([P, I], U32, name="wc", align_bytes=64)
+        wsc = sb.tile([P, I], U8, name="wsc", align_bytes=64)
+        yb = sb.tile([P, I, PACK], BF16, name="yb", align_bytes=64)
+        yc = sb.tile([P, I], U32, name="yc", align_bytes=64)
+        ysc = sb.tile([P, I], U8, name="ysc", align_bytes=64)
+        prob = sb.tile([P, PACK, I], F32, name="prob")
+        wrow = sb.tile([P, PACK, I], BF16, name="wrow")
+        nmax = sb.tile([P, PACK], F32, name="nmax", tag="early")
+        rsum = sb.tile([P, PACK], F32, name="rsum")
+        rinv = sb.tile([P, PACK], F32, name="rinv")
+        fac = sb.tile([P, PACK], F32, name="fac")
+        y = sb.tile([P, PACK, I], F32, name="y")
+        x = sb.tile([P, PACK, I], F32, name="x")
+        sq = sb.tile([P, PACK, I], F32, name="sq")
+        ssq = sb.tile([P, PACK, G], F32, name="ssq")
+        r2 = sb.tile([P, PACK, G], F32, name="r2")
+        rg = sb.tile([P, PACK, G], F32, name="rg")
+        amp = sb.tile([P, PACK, I], F32, name="amp")
+        cx = sb.tile([P, PACK, I], F32, name="cx")
+        pg = sb.tile([P, PACK, G], F32, name="pg")
+        kk = sb.tile([P, PACK, G], F32, name="kk")
+        xk = sb.tile([P, PACK, I], F32, name="xk")
+        u = sb.tile([P, PACK, I], F32, name="u")
+        ua = sb.tile([P, PACK, I], F32, name="ua")
+        score = [ps.tile([P, I], F32, name=f"s{t}") for t in range(PACK)]
+        tick = sb.tile([P, 8], F32, name="tick")
+
+        def clock(ap):
+            nc.gpsimd.tensor_copy(out=tick[:, 0:1], in_=ap)
+
+        def pages(tile, a, b):
+            return tile[:, a:b, :].rearrange("p t (g j) -> p t g j", j=PAGE)
+
+        def per_page(tile, a, b):
+            return tile[:, a:b, :].unsqueeze(3).to_broadcast([P, b - a, G, PAGE])
+
+        def gather_keys():
+            nc.vector.tensor_copy(kg[:], kw[:].indirect(offsets[:]))
+            nc.vector.tensor_copy(ksg[:], ks[:].indirect(offsets[:]))
+
+        def quant_q(a, b):
+            cols = slice(P * a, P * b)
+            quantize(qc[:, cols], qsc[:, cols], qb[:, a:b].rearrange("p t m j -> p (t m j)"))
+            for t in range(a, b):
+                cols = slice(P * t, P * (t + 1))
+                nc.tensor.matmul_mx(
+                    out=score[t][:], lhsT=qc[:, cols].bitcast(FP8X4), lhsT_scale=qsc[:, cols],
+                    rhs=kg[:].bitcast(FP8X4), rhs_scale=ksg[:], start=True, stop=True,
+                )
+
+        def softmax(t):
+            nc.vector.tensor_reduce(out=nmax[:, t : t + 1], in_=score[t][:], axis=AX.X, op=ALU.max, negate=True)
+            nc.scalar.activation(
+                out=prob[:, t, :], in_=score[t][:], func=ACT.Exp, bias=nmax[:, t : t + 1], scale=1.0,
+                accum_out=rsum[:, t : t + 1],
+            )
+
+        def factors(a, b):
+            nc.vector.reciprocal(out=rinv[:, a:b], in_=rsum[:, a:b])
+            nc.vector.tensor_tensor(out=fac[:, a:b], in0=rinv[:, a:b], in1=qs_col[:, a:b], op=ALU.mult)
+
+        def weights_v():
+            nc.vector.tensor_tensor(
+                out=wb[:], in0=prob[:].rearrange("p t i -> p i t"),
+                in1=fac[:].unsqueeze(1).to_broadcast([P, I, PACK]), op=ALU.mult,
+            )
+
+        def weights_s(t):
+            nc.scalar.activation(out=wrow[:, t, :], in_=prob[:, t, :], func=ACT.Copy, scale=fac[:, t : t + 1])
+
+        def weave_w():
+            nc.vector.tensor_copy(
+                out=wb[:].rearrange("p (c i) t -> p c t i", i=4), in_=wrow[:].rearrange("p t (c i) -> p c t i", i=4)
+            )
+
+        def quant_w():
+            quantize(wc[:], wsc[:], wb[:].rearrange("p i t -> p (i t)"))
+
+        def quant_g(a, b):
+            cols = slice(P * a, P * b)
+            quantize(gc[:, cols], gsc[:, cols], gb[:, a:b].rearrange("p t m j -> p (t m j)"))
+
+        def gather_x(t):
+            nc.vector.tensor_tensor(x[:, t, :], v_raw[t][:].indirect(offsets[:]), pre_row, ALU.mult)
+
+        def square(a, b):
+            nc.scalar.activation(out=sq[:, a:b, :], in_=x[:, a:b, :], func=ACT.Square)
+
+        def sum_sq(a, b):
+            nc.vector.tensor_reduce(out=ssq[:, a:b, :], in_=pages(sq, a, b), axis=AX.X, op=ALU.add)
+
+        held = {}
+
+        def norm(a, b):
+            if "rm" not in held:
+                held["rm"] = sb.tile([P, PACK, G], F32, name="rm", tag="graw")
+            rm = held["rm"]
+            nc.scalar.activation(
+                out=rm[:, a:b, :], in_=ssq[:, a:b, :], func=ACT.Abs_reciprocal_sqrt, scale=1.0 / PAGE, bias=0.05
+            )
+            for t in range(a, b):
+                nc.scalar.activation(out=rg[:, t, :], in_=rm[:, t, :], func=ACT.Copy, scale=gain_col[:, t : t + 1])
+            nc.scalar.activation(out=r2[:, a:b, :], in_=rm[:, a:b, :], func=ACT.Square, scale=0.25)
+
+        def amplitude(engine, a, b):
+            sg_pages = sg_row.rearrange("p (g j) -> p g j", j=PAGE).unsqueeze(1).to_broadcast([P, b - a, G, PAGE])
+            engine.tensor_tensor(out=pages(amp, a, b), in0=sg_pages, in1=per_page(rg, a, b), op=ALU.mult)
+
+        def amplitude_s(a, b):
+            for t in range(a, b):
+                for g in range(G):
+                    cols = slice(PAGE * g, PAGE * (g + 1))
+                    nc.scalar.activation(out=amp[:, t, cols], in_=sg_row[:, cols], func=ACT.Copy, scale=rg[:, t, g : g + 1])
+
+        c0 = []
+
+        def second_product(h):
+            c0.append(ps.tile([P, 2, I], F32, name=f"c{h}", tag=f"c{h}"))
+            for t in range(2 * h, 2 * h + 2):
+                cols = slice(P * t, P * (t + 1))
+                nc.tensor.matmul_mx(
+                    out=c0[h][:, t % 2, :], lhsT=gc[:, cols].bitcast(FP8X4), lhsT_scale=gsc[:, cols],
+                    rhs=wc[:].bitcast(FP8X4), rhs_scale=wsc[:], start=True, stop=True,
+                )
+
+        def c0_of(a, b):
+            return c0[a // 2][:, a % 2 : a % 2 + b - a, :]
+
+        def e_cx(a, b):
+            nc.vector.tensor_tensor(out=cx[:, a:b, :], in0=c0_of(a, b), in1=x[:, a:b, :], op=ALU.mult)
+
+        def e_sum(a, b):
+            nc.vector.tensor_reduce(out=pg[:, a:b, :], in_=pages(cx, a, b), axis=AX.X, op=ALU.add)
+
+        def e_k(a, b):
+            nc.vector.tensor_tensor(out=kk[:, a:b, :], in0=pg[:, a:b, :], in1=r2[:, a:b, :], op=ALU.mult)
+
+        def e_xk_s(a, b):
+            for t in range(a, b):
+                for g in range(G):
+                    cols = slice(PAGE * g, PAGE * (g + 1))
+                    nc.scalar.activation(out=xk[:, t, cols], in_=x[:, t, cols], func=ACT.Copy, scale=kk[:, t, g : g + 1])
+
+        def e_xk(engine, a, b):
+            engine.tensor_tensor(out=pages(xk, a, b), in0=pages(x, a, b), in1=per_page(kk, a, b), op=ALU.mult)
+
+        def e_u(a, b):
+            nc.vector.tensor_tensor(out=u[:, a:b, :], in0=c0_of(a, b), in1=xk[:, a:b, :], op=ALU.subtract)
+
+        def e_ua(a, b):
+            nc.vector.tensor_tensor(out=ua[:, a:b, :], in0=u[:, a:b, :], in1=amp[:, a:b, :], op=ALU.mult)
+
+        def e_y(engine, a, b):
+            engine.tensor_tensor(out=y[:, a:b, :], in0=ua[:, a:b, :], in1=old_sb[:, a:b, :], op=ALU.add)
+            nc.sync.dma_start(out=out_0.rearrange("(p t) i -> p t i", t=PACK)[:, a:b, :], in_=y[:, a:b, :])
+
+        def y_pair(engine, a):
+            out = yb[:, :, 2 * a : 2 * a + 2].rearrange("p (c i) t -> p c t i", i=4)
+            in_ = y[:, 2 * a : 2 * a + 2, :].rearrange("p t (c i) -> p c t i", i=4)
+            if engine == "v":
+                nc.vector.tensor_copy(out=out, in_=in_)
+            else:
+                nc.scalar.copy(out=out, in_=in_)
+
+        def planes():
+            quantize(yc[:], ysc[:], yb[:].rearrange("p i t -> p (i t)"))
+            nc.sync.dma_start(out=out_1[0].rearrange("p c r -> p (c r)").bitcast(I32), in_=yc[:].bitcast(I32))
+            for quad in range(4):
+                queue = nc.scalar if quad % 2 == 0 else nc.sync
+                queue.dma_start(
+                    out=out_2[0, 4 * quad : 4 * quad + 4, :].bitcast(I32),
+                    in_=ysc[32 * quad : 32 * quad + 4, :].bitcast(I32),
+                )
+
+        deal("v", qb, q_raw[0], 0, 64)
+        deal("v", qb, q_raw[1], 64, 106, 64)
+        deal("s", qb, q_raw[1], 106, 128, 64)
+        gather_keys()
+        quant_q(0, 2)
+        quant_q(2, 4)
+        spread_row(0, pre_col)
+        for t in range(PACK):
+            softmax(t)
+        factors(0, 4)
+        weights_v()
+        quant_w()
+        deal("s", gb, g_raw, 0, 128)
+        quant_g(0, 2)
+        second_product(0)
+        quant_g(2, 4)
+        second_product(1)
+        spread_row(1, sg_col)
+        gather_x(0)
+        gather_x(1)
+        square(0, 2)
+        sum_sq(0, 2)
+        norm(0, 2)
+        amplitude(nc.gpsimd, 0, 2)
+        gather_x(2)
+        gather_x(3)
+        square(2, 4)
+        sum_sq(2, 4)
+        norm(2, 4)
+        amplitude(nc.gpsimd, 2, 4)
+        e_cx(0, 2)
+        e_sum(0, 2)
+        e_cx(2, 4)
+        e_k(0, 2)
+        e_sum(2, 4)
+        e_xk(nc.vector, 0, 2)
+        e_k(2, 4)
+        e_xk_s(2, 4)
+        e_u(0, 2)
+        e_ua(0, 2)
+        e_u(2, 3)
+        e_y(nc.vector, 0, 2)
+        y_pair("s", 0)
+        e_u(3, 4)
+        e_ua(2, 3)
+        e_ua(3, 4)
+        e_y(nc.vector, 2, 3)
+        e_y(nc.vector, 3, 4)
+        y_pair("v", 1)
+        planes()

@@ -44,6 +44,9 @@ def tile_attend_bvpagescaled_d_pl_kernel(
 
         v_rows = vals.rearrange("(p t) c -> p t c", t=PACK)
 
+        def load_offs():
+            nc.sync.dma_start(offsets[:], offs)
+
         def load_kw():
             nc.sync.dma_start(out=kw[:].bitcast(I32), in_=keys_words[0].rearrange("p c r -> p (c r)").bitcast(I32))
 
@@ -80,18 +83,18 @@ def tile_attend_bvpagescaled_d_pl_kernel(
             nc.sync.dma_start(out=gain_col[:], in_=gain.rearrange("(p t) o -> p (t o)", t=PACK))
 
         nc.gpsimd.memset(ks[:].bitcast(I32), 0)
-        nc.sync.dma_start(offsets[:], offs)
-        load_ks()
-        load_pre()
         load_q(0)
+        load_offs()
+        load_ks()
         load_kw()
         load_q(1)
-        load_qs()
-        load_v(0)
-        load_g()
+        load_pre()
         load_sg()
-        load_gain()
+        load_v(0)
+        load_qs()
         load_v(1)
+        load_g()
+        load_gain()
         load_v(2)
         load_v(3)
         load_old()
@@ -172,6 +175,62 @@ def tile_attend_bvpagescaled_d_pl_kernel(
         def gather_keys():
             nc.vector.tensor_copy(kg[:], kw[:].indirect(offsets[:]))
             nc.vector.tensor_copy(ksg[:], ks[:].indirect(offsets[:]))
+
+        def gather_kw():
+            nc.vector.tensor_copy(kg[:], kw[:].indirect(offsets[:]))
+
+        def gather_ks():
+            nc.vector.tensor_copy(ksg[:], ks[:].indirect(offsets[:]))
+
+        def recip(a, b):
+            nc.vector.reciprocal(out=rinv[:, a:b], in_=rsum[:, a:b])
+
+        def weights_t(t):
+            nc.vector.tensor_scalar(
+                out=wrow[:, t, :], in0=prob[:, t, :], scalar1=rinv[:, t : t + 1], scalar2=qs_col[:, t : t + 1],
+                op0=ALU.mult, op1=ALU.mult,
+            )
+
+        HALF = I // 2
+
+        def h_xk_s(h):
+            for t in (2, 3):
+                for g in range(h * G // 2, (h + 1) * G // 2):
+                    cols = slice(PAGE * g, PAGE * (g + 1))
+                    nc.scalar.activation(out=xk[:, t, cols], in_=x[:, t, cols], func=ACT.Copy, scale=kk[:, t, g : g + 1])
+
+        def h_u(h):
+            cols = slice(h * HALF, (h + 1) * HALF)
+            nc.vector.tensor_tensor(out=u[:, 2:4, cols], in0=c0[1][:, :, cols], in1=xk[:, 2:4, cols], op=ALU.subtract)
+
+        def h_ua(h):
+            cols = slice(h * HALF, (h + 1) * HALF)
+            nc.vector.tensor_tensor(out=ua[:, 2:4, cols], in0=u[:, 2:4, cols], in1=amp[:, 2:4, cols], op=ALU.mult)
+
+        def h_y(h):
+            cols = slice(h * HALF, (h + 1) * HALF)
+            nc.vector.tensor_tensor(out=y[:, 2:4, cols], in0=ua[:, 2:4, cols], in1=old_sb[:, 2:4, cols], op=ALU.add)
+
+        def store_y(a, b):
+            nc.sync.dma_start(out=out_0.rearrange("(p t) i -> p t i", t=PACK)[:, a:b, :], in_=y[:, a:b, :])
+
+        def h_cast(h):
+            cols = slice(h * HALF, (h + 1) * HALF)
+            out = yb[:, cols, 2:4].rearrange("p (c i) t -> p c t i", i=4)
+            nc.vector.tensor_copy(out=out, in_=y[:, 2:4, cols].rearrange("p t (c i) -> p c t i", i=4))
+
+        def h_quant(h):
+            cols = slice(h * HALF, (h + 1) * HALF)
+            quantize(yc[:, cols], ysc[:, cols], yb[:, cols, :].rearrange("p i t -> p (i t)"))
+
+        def store_planes():
+            nc.sync.dma_start(out=out_1[0].rearrange("p c r -> p (c r)").bitcast(I32), in_=yc[:].bitcast(I32))
+            for quad in range(4):
+                queue = nc.scalar if quad % 2 == 0 else nc.sync
+                queue.dma_start(
+                    out=out_2[0, 4 * quad : 4 * quad + 4, :].bitcast(I32),
+                    in_=ysc[32 * quad : 32 * quad + 4, :].bitcast(I32),
+                )
 
         def quant_q(a, b):
             cols = slice(P * a, P * b)
@@ -308,52 +367,66 @@ def tile_attend_bvpagescaled_d_pl_kernel(
                 )
 
         deal("v", qb, q_raw[0], 0, 64)
+        gather_ks()
+        gather_kw()
         deal("v", qb, q_raw[1], 64, 106, 64)
         deal("s", qb, q_raw[1], 106, 128, 64)
-        gather_keys()
+        spread_row(0, pre_col)
         quant_q(0, 2)
         quant_q(2, 4)
-        spread_row(0, pre_col)
+        spread_row(1, sg_col)
         for t in range(PACK):
             softmax(t)
-        factors(0, 4)
-        weights_v()
+        recip(0, 2)
+        weights_t(0)
+        weights_t(1)
+        recip(2, 4)
+        weights_t(2)
+        weights_t(3)
+        weave_w()
         quant_w()
         deal("s", gb, g_raw, 0, 128)
         quant_g(0, 2)
         second_product(0)
         quant_g(2, 4)
         second_product(1)
-        spread_row(1, sg_col)
         gather_x(0)
         gather_x(1)
         square(0, 2)
         sum_sq(0, 2)
         norm(0, 2)
-        amplitude(nc.gpsimd, 0, 2)
+        amplitude(nc.gpsimd, 0, 1)
+        amplitude(nc.gpsimd, 1, 2)
         gather_x(2)
         gather_x(3)
         square(2, 4)
+        e_cx(0, 2)
+        e_cx(2, 4)
         sum_sq(2, 4)
         norm(2, 4)
-        amplitude(nc.gpsimd, 2, 4)
-        e_cx(0, 2)
+        amplitude(nc.gpsimd, 2, 3)
+        amplitude(nc.gpsimd, 3, 4)
         e_sum(0, 2)
-        e_cx(2, 4)
-        e_k(0, 2)
         e_sum(2, 4)
-        e_xk(nc.vector, 0, 2)
-        e_k(2, 4)
+        e_k(0, 4)
         e_xk_s(2, 4)
-        e_u(0, 2)
-        e_ua(0, 2)
-        e_u(2, 3)
-        e_y(nc.vector, 0, 2)
+        e_xk(nc.vector, 0, 1)
+        e_xk(nc.vector, 1, 2)
+        e_u(0, 1)
+        e_u(1, 2)
+        e_ua(0, 1)
+        e_ua(1, 2)
+        e_u(2, 4)
+        e_y(nc.vector, 0, 1)
+        e_y(nc.vector, 1, 2)
         y_pair("s", 0)
-        e_u(3, 4)
-        e_ua(2, 3)
-        e_ua(3, 4)
-        e_y(nc.vector, 2, 3)
-        e_y(nc.vector, 3, 4)
-        y_pair("v", 1)
-        planes()
+        h_ua(0)
+        h_ua(1)
+        h_y(0)
+        h_y(1)
+        store_y(2, 4)
+        h_cast(0)
+        h_cast(1)
+        h_quant(0)
+        h_quant(1)
+        store_planes()

@@ -5,9 +5,12 @@ from concourse.masks import make_identity
 
 D, E, T, I, Q, G = 512, 512, 1024, 256, 512, 16
 PAGE = I // G
+HALF = I // 2
 P = 128
 PACK = 4
+EPS = 0.05
 FLOPS = 2 * D * Q * I + 2 * Q * E * I
+VECTOR_GROUPS = 42
 
 F32 = mybir.dt.float32
 BF16 = mybir.dt.bfloat16
@@ -42,91 +45,42 @@ def tile_attend_bvpagescaled_d_pl_kernel(
         gain_col = sb.tile([P, PACK], F32, name="gain_col")
         ident = sb.tile([P, P], F32, name="ident")
 
+        q_rows = query.rearrange("(p j) q -> p j q", j=PACK)
         v_rows = vals.rearrange("(p t) c -> p t c", t=PACK)
-
-        def load_offs():
-            nc.sync.dma_start(offsets[:], offs)
-
-        def load_kw():
-            nc.sync.dma_start(out=kw[:].bitcast(I32), in_=keys_words[0].rearrange("p c r -> p (c r)").bitcast(I32))
+        out_rows = out_0.rearrange("(p t) i -> p t i", t=PACK)
 
         def load_q(h):
-            cols = slice(h * Q // 2, (h + 1) * Q // 2)
-            nc.sync.dma_start(out=q_raw[h][:], in_=query.rearrange("(p j) q -> p j q", j=PACK)[:, :, cols])
-
-        def load_g():
-            nc.sync.dma_start(out=g_raw[:], in_=grows.rearrange("(p j) e -> p j e", j=PACK))
+            nc.sync.dma_start(out=q_raw[h][:], in_=q_rows[:, :, h * Q // 2 : (h + 1) * Q // 2])
 
         def load_v(t):
             nc.sync.dma_start(out=v_raw[t][:], in_=v_rows[:, t, :])
 
-        def load_old():
-            nc.sync.dma_start(out=old_sb[:], in_=old.rearrange("(p t) i -> p t i", t=PACK))
-
-        def load_ks():
-            for quad in range(4):
-                nc.sync.dma_start(
-                    out=ks[32 * quad : 32 * quad + 4, :].bitcast(I32),
-                    in_=keys_scales[0, 4 * quad : 4 * quad + 4, :].bitcast(I32),
-                )
-
-        def load_pre():
-            nc.sync.dma_start(out=pre_col[:], in_=pre.rearrange("o (p h) -> p (o h)", h=2))
-
-        def load_sg():
-            nc.sync.dma_start(out=sg_col[:], in_=sg.rearrange("o (p h) -> p (o h)", h=2))
-
-        def load_qs():
-            nc.sync.dma_start(out=qs_col[:], in_=qs.rearrange("(p t) o -> p (t o)", t=PACK))
-
-        def load_gain():
-            nc.sync.dma_start(out=gain_col[:], in_=gain.rearrange("(p t) o -> p (t o)", t=PACK))
-
         nc.gpsimd.memset(ks[:].bitcast(I32), 0)
+
         load_q(0)
-        load_offs()
-        load_ks()
-        load_kw()
+        nc.sync.dma_start(offsets[:], offs)
+        for quad in range(4):
+            nc.sync.dma_start(
+                out=ks[32 * quad : 32 * quad + 4, :].bitcast(I32),
+                in_=keys_scales[0, 4 * quad : 4 * quad + 4, :].bitcast(I32),
+            )
+        nc.sync.dma_start(out=kw[:].bitcast(I32), in_=keys_words[0].rearrange("p c r -> p (c r)").bitcast(I32))
         load_q(1)
-        load_pre()
-        load_sg()
+        nc.sync.dma_start(out=pre_col[:], in_=pre.rearrange("o (p h) -> p (o h)", h=2))
+        nc.sync.dma_start(out=sg_col[:], in_=sg.rearrange("o (p h) -> p (o h)", h=2))
         load_v(0)
-        load_qs()
+        nc.sync.dma_start(out=qs_col[:], in_=qs.rearrange("(p t) o -> p (t o)", t=PACK))
         load_v(1)
-        load_g()
-        load_gain()
+        nc.sync.dma_start(out=g_raw[:], in_=grows.rearrange("(p j) e -> p j e", j=PACK))
+        nc.sync.dma_start(out=gain_col[:], in_=gain.rearrange("(p t) o -> p (t o)", t=PACK))
         load_v(2)
         load_v(3)
-        load_old()
+        nc.sync.dma_start(out=old_sb[:], in_=old.rearrange("(p t) i -> p t i", t=PACK))
         make_identity(nc, ident[:])
 
         rows = sb.tile([P, 2, I], F32, name="rows")
         pre_row = rows[:, 0, :]
         sg_row = rows[:, 1, :]
-
-        def spread_row(v, col):
-            spread = ps.tile([P, 2, P], F32, name=f"spread{v}")
-            for h in range(2):
-                nc.tensor.transpose(spread[:, h, :], col[:, h : h + 1].to_broadcast([P, P]), ident[:])
-            nc.scalar.activation(
-                out=rows[:, v, :].rearrange("p (i h) -> p i h", h=2),
-                in_=spread[:].rearrange("p h i -> p i h"),
-                func=ACT.Copy,
-            )
-
-        def deal(engine, dst, src, lo, hi, base=0):
-            out = dst[:, :, lo:hi, :].rearrange("p t m j -> p m j t")
-            in_ = src[:, :, PACK * (lo - base) : PACK * (hi - base)].rearrange("p j (m t) -> p m j t", t=PACK)
-            if engine == "v":
-                nc.vector.tensor_copy(out=out, in_=in_)
-            elif engine == "g":
-                nc.gpsimd.tensor_scalar(out=out, in0=in_, scalar1=1.0, scalar2=0.0, op0=ALU.mult, op1=ALU.add)
-            else:
-                nc.scalar.copy(out=out, in_=in_)
-
-        def quantize(codes, scales, src):
-            nc.vector.quantize_mx(out=codes.bitcast(FP8X4), scales=scales, in_=src)
-
         kg = sb.tile([P, I], U32, name="kg", align_bytes=64)
         ksg = sb.tile([P, I], U8, name="ksg", align_bytes=64)
         qb = sb.tile([P, PACK, P, PACK], BF16, name="qb", align_bytes=64)
@@ -143,10 +97,9 @@ def tile_attend_bvpagescaled_d_pl_kernel(
         ysc = sb.tile([P, I], U8, name="ysc", align_bytes=64)
         prob = sb.tile([P, PACK, I], F32, name="prob")
         wrow = sb.tile([P, PACK, I], BF16, name="wrow")
-        nmax = sb.tile([P, PACK], F32, name="nmax", tag="early")
+        nmax = sb.tile([P, PACK], F32, name="nmax")
         rsum = sb.tile([P, PACK], F32, name="rsum")
         rinv = sb.tile([P, PACK], F32, name="rinv")
-        fac = sb.tile([P, PACK], F32, name="fac")
         y = sb.tile([P, PACK, I], F32, name="y")
         x = sb.tile([P, PACK, I], F32, name="x")
         sq = sb.tile([P, PACK, I], F32, name="sq")
@@ -155,16 +108,12 @@ def tile_attend_bvpagescaled_d_pl_kernel(
         rg = sb.tile([P, PACK, G], F32, name="rg")
         amp = sb.tile([P, PACK, I], F32, name="amp")
         cx = sb.tile([P, PACK, I], F32, name="cx")
-        pg = sb.tile([P, PACK, G], F32, name="pg")
-        kk = sb.tile([P, PACK, G], F32, name="kk")
-        xk = sb.tile([P, PACK, I], F32, name="xk")
-        u = sb.tile([P, PACK, I], F32, name="u")
-        ua = sb.tile([P, PACK, I], F32, name="ua")
-        score = [ps.tile([P, I], F32, name=f"s{t}") for t in range(PACK)]
-        tick = sb.tile([P, 8], F32, name="tick")
-
-        def clock(ap):
-            nc.gpsimd.tensor_copy(out=tick[:, 0:1], in_=ap)
+        cx_sum = sb.tile([P, PACK, G], F32, name="cx_sum")
+        coef = sb.tile([P, PACK, G], F32, name="coef")
+        x_coef = sb.tile([P, PACK, I], F32, name="x_coef")
+        diff = sb.tile([P, PACK, I], F32, name="diff")
+        scaled = sb.tile([P, PACK, I], F32, name="scaled")
+        score = [ps.tile([P, I], F32, name=f"score{t}") for t in range(PACK)]
 
         def pages(tile, a, b):
             return tile[:, a:b, :].rearrange("p t (g j) -> p t g j", j=PAGE)
@@ -172,261 +121,147 @@ def tile_attend_bvpagescaled_d_pl_kernel(
         def per_page(tile, a, b):
             return tile[:, a:b, :].unsqueeze(3).to_broadcast([P, b - a, G, PAGE])
 
-        def gather_keys():
-            nc.vector.tensor_copy(kg[:], kw[:].indirect(offsets[:]))
-            nc.vector.tensor_copy(ksg[:], ks[:].indirect(offsets[:]))
+        def deal(copy, dst, src):
+            copy(out=dst.rearrange("p t m j -> p m j t"), in_=src.rearrange("p j (m t) -> p m j t", t=PACK))
 
-        def gather_kw():
-            nc.vector.tensor_copy(kg[:], kw[:].indirect(offsets[:]))
+        def weave(copy, dst, src):
+            copy(out=dst.rearrange("p (c i) t -> p c t i", i=4), in_=src.rearrange("p t (c i) -> p c t i", i=4))
 
-        def gather_ks():
-            nc.vector.tensor_copy(ksg[:], ks[:].indirect(offsets[:]))
+        def quantize(codes, scales, src):
+            nc.vector.quantize_mx(out=codes.bitcast(FP8X4), scales=scales, in_=src)
 
-        def recip(a, b):
-            nc.vector.reciprocal(out=rinv[:, a:b], in_=rsum[:, a:b])
-
-        def weights_t(t):
-            nc.vector.tensor_scalar(
-                out=wrow[:, t, :], in0=prob[:, t, :], scalar1=rinv[:, t : t + 1], scalar2=qs_col[:, t : t + 1],
-                op0=ALU.mult, op1=ALU.mult,
+        def product(out, codes, scales, t, moving, moving_scales):
+            cols = slice(P * t, P * (t + 1))
+            nc.tensor.matmul_mx(
+                out=out, lhsT=codes[:, cols].bitcast(FP8X4), lhsT_scale=scales[:, cols],
+                rhs=moving[:].bitcast(FP8X4), rhs_scale=moving_scales[:], start=True, stop=True,
             )
 
-        HALF = I // 2
+        def spread_row(row, col, name):
+            spread = ps.tile([P, 2, P], F32, name=name)
+            for h in range(2):
+                nc.tensor.transpose(spread[:, h, :], col[:, h : h + 1].to_broadcast([P, P]), ident[:])
+            nc.scalar.activation(
+                out=row.rearrange("p (i h) -> p i h", h=2), in_=spread[:].rearrange("p h i -> p i h"), func=ACT.Copy
+            )
 
-        def h_xk_s(h):
-            for t in (2, 3):
-                for g in range(h * G // 2, (h + 1) * G // 2):
+        def scale_pages_on_scalar(dst, src_of, factors, a, b):
+            for t in range(a, b):
+                for g in range(G):
                     cols = slice(PAGE * g, PAGE * (g + 1))
-                    nc.scalar.activation(out=xk[:, t, cols], in_=x[:, t, cols], func=ACT.Copy, scale=kk[:, t, g : g + 1])
+                    nc.scalar.activation(
+                        out=dst[:, t, cols], in_=src_of(t)[:, cols], func=ACT.Copy, scale=factors[:, t, g : g + 1]
+                    )
 
-        def h_u(h):
-            cols = slice(h * HALF, (h + 1) * HALF)
-            nc.vector.tensor_tensor(out=u[:, 2:4, cols], in0=c0[1][:, :, cols], in1=xk[:, 2:4, cols], op=ALU.subtract)
-
-        def h_ua(h):
-            cols = slice(h * HALF, (h + 1) * HALF)
-            nc.vector.tensor_tensor(out=ua[:, 2:4, cols], in0=u[:, 2:4, cols], in1=amp[:, 2:4, cols], op=ALU.mult)
-
-        def h_y(h):
-            cols = slice(h * HALF, (h + 1) * HALF)
-            nc.vector.tensor_tensor(out=y[:, 2:4, cols], in0=ua[:, 2:4, cols], in1=old_sb[:, 2:4, cols], op=ALU.add)
-
-        def store_y(a, b):
-            nc.sync.dma_start(out=out_0.rearrange("(p t) i -> p t i", t=PACK)[:, a:b, :], in_=y[:, a:b, :])
-
-        def h_cast(h):
-            cols = slice(h * HALF, (h + 1) * HALF)
-            out = yb[:, cols, 2:4].rearrange("p (c i) t -> p c t i", i=4)
-            nc.vector.tensor_copy(out=out, in_=y[:, 2:4, cols].rearrange("p t (c i) -> p c t i", i=4))
-
-        def h_quant(h):
-            cols = slice(h * HALF, (h + 1) * HALF)
-            quantize(yc[:, cols], ysc[:, cols], yb[:, cols, :].rearrange("p i t -> p (i t)"))
-
-        def store_planes():
-            nc.sync.dma_start(out=out_1[0].rearrange("p c r -> p (c r)").bitcast(I32), in_=yc[:].bitcast(I32))
-            for quad in range(4):
-                queue = nc.scalar if quad % 2 == 0 else nc.sync
-                queue.dma_start(
-                    out=out_2[0, 4 * quad : 4 * quad + 4, :].bitcast(I32),
-                    in_=ysc[32 * quad : 32 * quad + 4, :].bitcast(I32),
-                )
-
-        def quant_q(a, b):
+        middle = P // 2
+        split = middle + VECTOR_GROUPS
+        deal(nc.vector.tensor_copy, qb[:, :, :middle, :], q_raw[0][:])
+        nc.vector.tensor_copy(ksg[:], ks[:].indirect(offsets[:]))
+        nc.vector.tensor_copy(kg[:], kw[:].indirect(offsets[:]))
+        deal(nc.vector.tensor_copy, qb[:, :, middle:split, :], q_raw[1][:, :, : PACK * VECTOR_GROUPS])
+        deal(nc.scalar.copy, qb[:, :, split:, :], q_raw[1][:, :, PACK * VECTOR_GROUPS :])
+        spread_row(pre_row, pre_col, "spread_pre")
+        for a, b in ((0, 2), (2, 4)):
             cols = slice(P * a, P * b)
             quantize(qc[:, cols], qsc[:, cols], qb[:, a:b].rearrange("p t m j -> p (t m j)"))
             for t in range(a, b):
-                cols = slice(P * t, P * (t + 1))
-                nc.tensor.matmul_mx(
-                    out=score[t][:], lhsT=qc[:, cols].bitcast(FP8X4), lhsT_scale=qsc[:, cols],
-                    rhs=kg[:].bitcast(FP8X4), rhs_scale=ksg[:], start=True, stop=True,
-                )
+                product(score[t][:], qc, qsc, t, kg, ksg)
+        spread_row(sg_row, sg_col, "spread_sg")
 
-        def softmax(t):
+        for t in range(PACK):
             nc.vector.tensor_reduce(out=nmax[:, t : t + 1], in_=score[t][:], axis=AX.X, op=ALU.max, negate=True)
             nc.scalar.activation(
                 out=prob[:, t, :], in_=score[t][:], func=ACT.Exp, bias=nmax[:, t : t + 1], scale=1.0,
                 accum_out=rsum[:, t : t + 1],
             )
+        for a in (0, 2):
+            nc.vector.reciprocal(out=rinv[:, a : a + 2], in_=rsum[:, a : a + 2])
+            for t in (a, a + 1):
+                nc.vector.tensor_scalar(
+                    out=wrow[:, t, :], in0=prob[:, t, :], scalar1=rinv[:, t : t + 1], scalar2=qs_col[:, t : t + 1],
+                    op0=ALU.mult, op1=ALU.mult,
+                )
+        weave(nc.vector.tensor_copy, wb[:], wrow[:])
+        quantize(wc[:], wsc[:], wb[:].rearrange("p i t -> p (i t)"))
 
-        def factors(a, b):
-            nc.vector.reciprocal(out=rinv[:, a:b], in_=rsum[:, a:b])
-            nc.vector.tensor_tensor(out=fac[:, a:b], in0=rinv[:, a:b], in1=qs_col[:, a:b], op=ALU.mult)
+        deal(nc.scalar.copy, gb[:], g_raw[:])
+        c0 = []
+        for pair in range(2):
+            cols = slice(2 * P * pair, 2 * P * (pair + 1))
+            quantize(gc[:, cols], gsc[:, cols], gb[:, 2 * pair : 2 * pair + 2].rearrange("p t m j -> p (t m j)"))
+            c0.append(ps.tile([P, 2, I], F32, name=f"c0_{pair}"))
+            for s in range(2):
+                product(c0[pair][:, s, :], gc, gsc, 2 * pair + s, wc, wsc)
 
-        def weights_v():
-            nc.vector.tensor_tensor(
-                out=wb[:], in0=prob[:].rearrange("p t i -> p i t"),
-                in1=fac[:].unsqueeze(1).to_broadcast([P, I, PACK]), op=ALU.mult,
-            )
-
-        def weights_s(t):
-            nc.scalar.activation(out=wrow[:, t, :], in_=prob[:, t, :], func=ACT.Copy, scale=fac[:, t : t + 1])
-
-        def weave_w():
-            nc.vector.tensor_copy(
-                out=wb[:].rearrange("p (c i) t -> p c t i", i=4), in_=wrow[:].rearrange("p t (c i) -> p c t i", i=4)
-            )
-
-        def quant_w():
-            quantize(wc[:], wsc[:], wb[:].rearrange("p i t -> p (i t)"))
-
-        def quant_g(a, b):
-            cols = slice(P * a, P * b)
-            quantize(gc[:, cols], gsc[:, cols], gb[:, a:b].rearrange("p t m j -> p (t m j)"))
-
-        def gather_x(t):
-            nc.vector.tensor_tensor(x[:, t, :], v_raw[t][:].indirect(offsets[:]), pre_row, ALU.mult)
-
-        def square(a, b):
+        def gather_and_square(a, b):
+            for t in range(a, b):
+                nc.vector.tensor_tensor(x[:, t, :], v_raw[t][:].indirect(offsets[:]), pre_row, ALU.mult)
             nc.scalar.activation(out=sq[:, a:b, :], in_=x[:, a:b, :], func=ACT.Square)
 
-        def sum_sq(a, b):
-            nc.vector.tensor_reduce(out=ssq[:, a:b, :], in_=pages(sq, a, b), axis=AX.X, op=ALU.add)
+        def page_sum(dst, src, a, b):
+            nc.vector.tensor_reduce(out=dst[:, a:b, :], in_=pages(src, a, b), axis=AX.X, op=ALU.add)
 
-        held = {}
-
-        def norm(a, b):
-            if "rm" not in held:
-                held["rm"] = sb.tile([P, PACK, G], F32, name="rm", tag="graw")
-            rm = held["rm"]
+        def norms(a, b):
             nc.scalar.activation(
-                out=rm[:, a:b, :], in_=ssq[:, a:b, :], func=ACT.Abs_reciprocal_sqrt, scale=1.0 / PAGE, bias=0.05
+                out=rm[:, a:b, :], in_=ssq[:, a:b, :], func=ACT.Abs_reciprocal_sqrt, scale=1.0 / PAGE, bias=EPS
             )
             for t in range(a, b):
                 nc.scalar.activation(out=rg[:, t, :], in_=rm[:, t, :], func=ACT.Copy, scale=gain_col[:, t : t + 1])
-            nc.scalar.activation(out=r2[:, a:b, :], in_=rm[:, a:b, :], func=ACT.Square, scale=0.25)
+            nc.scalar.activation(out=r2[:, a:b, :], in_=rm[:, a:b, :], func=ACT.Square, scale=PAGE**-0.5)
 
-        def amplitude(engine, a, b):
-            sg_pages = sg_row.rearrange("p (g j) -> p g j", j=PAGE).unsqueeze(1).to_broadcast([P, b - a, G, PAGE])
-            engine.tensor_tensor(out=pages(amp, a, b), in0=sg_pages, in1=per_page(rg, a, b), op=ALU.mult)
+        gather_and_square(0, 2)
+        page_sum(ssq, sq, 0, 2)
+        rm = sb.tile([P, PACK, G], F32, name="rm", tag="graw")
+        norms(0, 2)
+        gather_and_square(2, 4)
 
-        def amplitude_s(a, b):
-            for t in range(a, b):
-                for g in range(G):
-                    cols = slice(PAGE * g, PAGE * (g + 1))
-                    nc.scalar.activation(out=amp[:, t, cols], in_=sg_row[:, cols], func=ACT.Copy, scale=rg[:, t, g : g + 1])
+        def mul(out, in0, in1):
+            nc.vector.tensor_tensor(out=out, in0=in0, in1=in1, op=ALU.mult)
 
-        c0 = []
+        mul(cx[:, 0:2, :], c0[0][:], x[:, 0:2, :])
+        page_sum(ssq, sq, 2, 4)
+        norms(2, 4)
+        scale_pages_on_scalar(amp, lambda t: sg_row, rg, 0, 2)
+        page_sum(cx_sum, cx, 0, 2)
+        mul(cx[:, 2:4, :], c0[1][:], x[:, 2:4, :])
+        mul(coef[:, 0:2, :], cx_sum[:, 0:2, :], r2[:, 0:2, :])
+        page_sum(cx_sum, cx, 2, 4)
+        mul(pages(x_coef, 0, 1), pages(x, 0, 1), per_page(coef, 0, 1))
+        mul(coef[:, 2:4, :], cx_sum[:, 2:4, :], r2[:, 2:4, :])
+        scale_pages_on_scalar(x_coef, lambda t: x[:, t, :], coef, 2, 4)
+        mul(pages(x_coef, 1, 2), pages(x, 1, 2), per_page(coef, 1, 2))
+        sg_pages = sg_row.rearrange("p (g j) -> p g j", j=PAGE).unsqueeze(1).to_broadcast([P, 2, G, PAGE])
+        mul(pages(amp, 2, 4), sg_pages, per_page(rg, 2, 4))
 
-        def second_product(h):
-            c0.append(ps.tile([P, 2, I], F32, name=f"c{h}", tag=f"c{h}"))
-            for t in range(2 * h, 2 * h + 2):
-                cols = slice(P * t, P * (t + 1))
-                nc.tensor.matmul_mx(
-                    out=c0[h][:, t % 2, :], lhsT=gc[:, cols].bitcast(FP8X4), lhsT_scale=gsc[:, cols],
-                    rhs=wc[:].bitcast(FP8X4), rhs_scale=wsc[:], start=True, stop=True,
-                )
+        for t in (0, 1):
+            nc.vector.tensor_tensor(
+                out=diff[:, t : t + 1, :], in0=c0[0][:, t : t + 1, :], in1=x_coef[:, t : t + 1, :], op=ALU.subtract
+            )
+        for t in (0, 1):
+            mul(scaled[:, t : t + 1, :], diff[:, t : t + 1, :], amp[:, t : t + 1, :])
+        nc.vector.tensor_tensor(out=diff[:, 2:4, :], in0=c0[1][:], in1=x_coef[:, 2:4, :], op=ALU.subtract)
+        for t in (0, 1):
+            nc.vector.tensor_tensor(
+                out=y[:, t : t + 1, :], in0=scaled[:, t : t + 1, :], in1=old_sb[:, t : t + 1, :], op=ALU.add
+            )
+            nc.sync.dma_start(out=out_rows[:, t : t + 1, :], in_=y[:, t : t + 1, :])
+        weave(nc.scalar.copy, yb[:, :, 0:2], y[:, 0:2, :])
 
-        def c0_of(a, b):
-            return c0[a // 2][:, a % 2 : a % 2 + b - a, :]
+        halves = [slice(h * HALF, (h + 1) * HALF) for h in range(2)]
+        for cols in halves:
+            mul(scaled[:, 2:4, cols], diff[:, 2:4, cols], amp[:, 2:4, cols])
+        for cols in halves:
+            nc.vector.tensor_tensor(out=y[:, 2:4, cols], in0=scaled[:, 2:4, cols], in1=old_sb[:, 2:4, cols], op=ALU.add)
+        nc.sync.dma_start(out=out_rows[:, 2:4, :], in_=y[:, 2:4, :])
+        for cols in halves:
+            weave(nc.vector.tensor_copy, yb[:, cols, 2:4], y[:, 2:4, cols])
+        for cols in halves:
+            quantize(yc[:, cols], ysc[:, cols], yb[:, cols, :].rearrange("p i t -> p (i t)"))
 
-        def e_cx(a, b):
-            nc.vector.tensor_tensor(out=cx[:, a:b, :], in0=c0_of(a, b), in1=x[:, a:b, :], op=ALU.mult)
-
-        def e_sum(a, b):
-            nc.vector.tensor_reduce(out=pg[:, a:b, :], in_=pages(cx, a, b), axis=AX.X, op=ALU.add)
-
-        def e_k(a, b):
-            nc.vector.tensor_tensor(out=kk[:, a:b, :], in0=pg[:, a:b, :], in1=r2[:, a:b, :], op=ALU.mult)
-
-        def e_xk_s(a, b):
-            for t in range(a, b):
-                for g in range(G):
-                    cols = slice(PAGE * g, PAGE * (g + 1))
-                    nc.scalar.activation(out=xk[:, t, cols], in_=x[:, t, cols], func=ACT.Copy, scale=kk[:, t, g : g + 1])
-
-        def e_xk(engine, a, b):
-            engine.tensor_tensor(out=pages(xk, a, b), in0=pages(x, a, b), in1=per_page(kk, a, b), op=ALU.mult)
-
-        def e_u(a, b):
-            nc.vector.tensor_tensor(out=u[:, a:b, :], in0=c0_of(a, b), in1=xk[:, a:b, :], op=ALU.subtract)
-
-        def e_ua(a, b):
-            nc.vector.tensor_tensor(out=ua[:, a:b, :], in0=u[:, a:b, :], in1=amp[:, a:b, :], op=ALU.mult)
-
-        def e_y(engine, a, b):
-            engine.tensor_tensor(out=y[:, a:b, :], in0=ua[:, a:b, :], in1=old_sb[:, a:b, :], op=ALU.add)
-            nc.sync.dma_start(out=out_0.rearrange("(p t) i -> p t i", t=PACK)[:, a:b, :], in_=y[:, a:b, :])
-
-        def y_pair(engine, a):
-            out = yb[:, :, 2 * a : 2 * a + 2].rearrange("p (c i) t -> p c t i", i=4)
-            in_ = y[:, 2 * a : 2 * a + 2, :].rearrange("p t (c i) -> p c t i", i=4)
-            if engine == "v":
-                nc.vector.tensor_copy(out=out, in_=in_)
-            else:
-                nc.scalar.copy(out=out, in_=in_)
-
-        def planes():
-            quantize(yc[:], ysc[:], yb[:].rearrange("p i t -> p (i t)"))
-            nc.sync.dma_start(out=out_1[0].rearrange("p c r -> p (c r)").bitcast(I32), in_=yc[:].bitcast(I32))
-            for quad in range(4):
-                queue = nc.scalar if quad % 2 == 0 else nc.sync
-                queue.dma_start(
-                    out=out_2[0, 4 * quad : 4 * quad + 4, :].bitcast(I32),
-                    in_=ysc[32 * quad : 32 * quad + 4, :].bitcast(I32),
-                )
-
-        deal("v", qb, q_raw[0], 0, 64)
-        gather_ks()
-        gather_kw()
-        deal("v", qb, q_raw[1], 64, 106, 64)
-        deal("s", qb, q_raw[1], 106, 128, 64)
-        spread_row(0, pre_col)
-        quant_q(0, 2)
-        quant_q(2, 4)
-        spread_row(1, sg_col)
-        for t in range(PACK):
-            softmax(t)
-        recip(0, 2)
-        weights_t(0)
-        weights_t(1)
-        recip(2, 4)
-        weights_t(2)
-        weights_t(3)
-        weave_w()
-        quant_w()
-        deal("s", gb, g_raw, 0, 128)
-        quant_g(0, 2)
-        second_product(0)
-        quant_g(2, 4)
-        second_product(1)
-        gather_x(0)
-        gather_x(1)
-        square(0, 2)
-        sum_sq(0, 2)
-        norm(0, 2)
-        amplitude(nc.gpsimd, 0, 1)
-        amplitude(nc.gpsimd, 1, 2)
-        gather_x(2)
-        gather_x(3)
-        square(2, 4)
-        e_cx(0, 2)
-        e_cx(2, 4)
-        sum_sq(2, 4)
-        norm(2, 4)
-        amplitude(nc.gpsimd, 2, 3)
-        amplitude(nc.gpsimd, 3, 4)
-        e_sum(0, 2)
-        e_sum(2, 4)
-        e_k(0, 4)
-        e_xk_s(2, 4)
-        e_xk(nc.vector, 0, 1)
-        e_xk(nc.vector, 1, 2)
-        e_u(0, 1)
-        e_u(1, 2)
-        e_ua(0, 1)
-        e_ua(1, 2)
-        e_u(2, 4)
-        e_y(nc.vector, 0, 1)
-        e_y(nc.vector, 1, 2)
-        y_pair("s", 0)
-        h_ua(0)
-        h_ua(1)
-        h_y(0)
-        h_y(1)
-        store_y(2, 4)
-        h_cast(0)
-        h_cast(1)
-        h_quant(0)
-        h_quant(1)
-        store_planes()
+        nc.sync.dma_start(out=out_1[0].rearrange("p c r -> p (c r)").bitcast(I32), in_=yc[:].bitcast(I32))
+        for quad in range(4):
+            queue = nc.scalar if quad % 2 == 0 else nc.sync
+            queue.dma_start(
+                out=out_2[0, 4 * quad : 4 * quad + 4, :].bitcast(I32),
+                in_=ysc[32 * quad : 32 * quad + 4, :].bitcast(I32),
+            )

from contextlib import ExitStack

import concourse.mybir as mybir
from concourse.masks import make_identity

D, E, T, I, Q, G = 512, 512, 1024, 256, 512, 16
PAGE = I // G
HALF = I // 2
P = 128
PACK = 4
EPS = 0.05
FLOPS = 2 * D * Q * I + 2 * Q * E * I
VECTOR_GROUPS = 42

F32 = mybir.dt.float32
BF16 = mybir.dt.bfloat16
I32 = mybir.dt.int32
U32 = mybir.dt.uint32
U16 = mybir.dt.uint16
U8 = mybir.dt.uint8
FP8X4 = mybir.dt.float8_e4m3fn_x4
ALU = mybir.AluOpType
ACT = mybir.ActivationFunctionType
AX = mybir.AxisListType


def tile_attend_bvpagescaled_d_pl_kernel(
    tc, query, qs, grows, vals, keys_words, keys_scales, gain, pre, sg, old, offs, out_0, out_1, out_2
):
    nc = tc.nc
    with ExitStack() as ctx:
        sb = ctx.enter_context(tc.tile_pool(name="sb", bufs=1))
        ps = ctx.enter_context(tc.psum_pool(name="ps", bufs=1))

        offsets = sb.tile([P, I // 16], U16, name="offsets")
        kw = sb.tile([P, T], U32, name="kw")
        ks = sb.tile([P, T], U8, name="ks")
        q_raw = [sb.tile([P, PACK, Q // 2], F32, name=f"q_raw{h}") for h in range(2)]
        g_raw = sb.tile([P, PACK, E], F32, name="g_raw", tag="graw")
        v_raw = [sb.tile([P, T], F32, name=f"v_raw{t}") for t in range(PACK)]
        old_sb = sb.tile([P, PACK, I], F32, name="old_sb")
        pre_col = sb.tile([P, 2], F32, name="pre_col")
        sg_col = sb.tile([P, 2], F32, name="sg_col")
        qs_col = sb.tile([P, PACK], F32, name="qs_col")
        gain_col = sb.tile([P, PACK], F32, name="gain_col")
        ident = sb.tile([P, P], F32, name="ident")

        q_rows = query.rearrange("(p j) q -> p j q", j=PACK)
        v_rows = vals.rearrange("(p t) c -> p t c", t=PACK)
        out_rows = out_0.rearrange("(p t) i -> p t i", t=PACK)

        def load_q(h):
            nc.sync.dma_start(out=q_raw[h][:], in_=q_rows[:, :, h * Q // 2 : (h + 1) * Q // 2])

        def load_v(t):
            nc.sync.dma_start(out=v_raw[t][:], in_=v_rows[:, t, :])

        nc.gpsimd.memset(ks[:].bitcast(I32), 0)

        load_q(0)
        nc.sync.dma_start(offsets[:], offs)
        for quad in range(4):
            nc.sync.dma_start(
                out=ks[32 * quad : 32 * quad + 4, :].bitcast(I32),
                in_=keys_scales[0, 4 * quad : 4 * quad + 4, :].bitcast(I32),
            )
        nc.sync.dma_start(out=kw[:].bitcast(I32), in_=keys_words[0].rearrange("p c r -> p (c r)").bitcast(I32))
        load_q(1)
        nc.sync.dma_start(out=pre_col[:], in_=pre.rearrange("o (p h) -> p (o h)", h=2))
        nc.sync.dma_start(out=sg_col[:], in_=sg.rearrange("o (p h) -> p (o h)", h=2))
        load_v(0)
        nc.sync.dma_start(out=qs_col[:], in_=qs.rearrange("(p t) o -> p (t o)", t=PACK))
        load_v(1)
        nc.sync.dma_start(out=g_raw[:], in_=grows.rearrange("(p j) e -> p j e", j=PACK))
        nc.sync.dma_start(out=gain_col[:], in_=gain.rearrange("(p t) o -> p (t o)", t=PACK))
        load_v(2)
        load_v(3)
        nc.sync.dma_start(out=old_sb[:], in_=old.rearrange("(p t) i -> p t i", t=PACK))
        make_identity(nc, ident[:])

        rows = sb.tile([P, 2, I], F32, name="rows")
        pre_row = rows[:, 0, :]
        sg_row = rows[:, 1, :]
        kg = sb.tile([P, I], U32, name="kg", align_bytes=64)
        ksg = sb.tile([P, I], U8, name="ksg", align_bytes=64)
        qb = sb.tile([P, PACK, P, PACK], BF16, name="qb", align_bytes=64)
        qc = sb.tile([P, Q], U32, name="qc", align_bytes=64)
        qsc = sb.tile([P, Q], U8, name="qsc", align_bytes=64)
        gb = sb.tile([P, PACK, P, PACK], BF16, name="gb", align_bytes=64)
        gc = sb.tile([P, E], U32, name="gc", align_bytes=64)
        gsc = sb.tile([P, E], U8, name="gsc", align_bytes=64)
        wb = sb.tile([P, I, PACK], BF16, name="wb", align_bytes=64)
        wc = sb.tile([P, I], U32, name="wc", align_bytes=64)
        wsc = sb.tile([P, I], U8, name="wsc", align_bytes=64)
        yb = sb.tile([P, I, PACK], BF16, name="yb", align_bytes=64)
        yc = sb.tile([P, I], U32, name="yc", align_bytes=64)
        ysc = sb.tile([P, I], U8, name="ysc", align_bytes=64)
        prob = sb.tile([P, PACK, I], F32, name="prob")
        wrow = sb.tile([P, PACK, I], BF16, name="wrow")
        nmax = sb.tile([P, PACK], F32, name="nmax")
        rsum = sb.tile([P, PACK], F32, name="rsum")
        rinv = sb.tile([P, PACK], F32, name="rinv")
        y = sb.tile([P, PACK, I], F32, name="y")
        x = sb.tile([P, PACK, I], F32, name="x")
        sq = sb.tile([P, PACK, I], F32, name="sq")
        ssq = sb.tile([P, PACK, G], F32, name="ssq")
        r2 = sb.tile([P, PACK, G], F32, name="r2")
        rg = sb.tile([P, PACK, G], F32, name="rg")
        amp = sb.tile([P, PACK, I], F32, name="amp")
        cx = sb.tile([P, PACK, I], F32, name="cx")
        cx_sum = sb.tile([P, PACK, G], F32, name="cx_sum")
        coef = sb.tile([P, PACK, G], F32, name="coef")
        x_coef = sb.tile([P, PACK, I], F32, name="x_coef")
        diff = sb.tile([P, PACK, I], F32, name="diff")
        scaled = sb.tile([P, PACK, I], F32, name="scaled")
        score = [ps.tile([P, I], F32, name=f"score{t}") for t in range(PACK)]

        def pages(tile, a, b):
            return tile[:, a:b, :].rearrange("p t (g j) -> p t g j", j=PAGE)

        def per_page(tile, a, b):
            return tile[:, a:b, :].unsqueeze(3).to_broadcast([P, b - a, G, PAGE])

        def deal(copy, dst, src):
            copy(out=dst.rearrange("p t m j -> p m j t"), in_=src.rearrange("p j (m t) -> p m j t", t=PACK))

        def weave(copy, dst, src):
            copy(out=dst.rearrange("p (c i) t -> p c t i", i=4), in_=src.rearrange("p t (c i) -> p c t i", i=4))

        def quantize(codes, scales, src):
            nc.vector.quantize_mx(out=codes.bitcast(FP8X4), scales=scales, in_=src)

        def product(out, codes, scales, t, moving, moving_scales):
            cols = slice(P * t, P * (t + 1))
            nc.tensor.matmul_mx(
                out=out, lhsT=codes[:, cols].bitcast(FP8X4), lhsT_scale=scales[:, cols],
                rhs=moving[:].bitcast(FP8X4), rhs_scale=moving_scales[:], start=True, stop=True,
            )

        def spread_row(row, col, name):
            spread = ps.tile([P, 2, P], F32, name=name)
            for h in range(2):
                nc.tensor.transpose(spread[:, h, :], col[:, h : h + 1].to_broadcast([P, P]), ident[:])
            nc.scalar.activation(
                out=row.rearrange("p (i h) -> p i h", h=2), in_=spread[:].rearrange("p h i -> p i h"), func=ACT.Copy
            )

        def scale_pages_on_scalar(dst, src_of, factors, a, b):
            for t in range(a, b):
                for g in range(G):
                    cols = slice(PAGE * g, PAGE * (g + 1))
                    nc.scalar.activation(
                        out=dst[:, t, cols], in_=src_of(t)[:, cols], func=ACT.Copy, scale=factors[:, t, g : g + 1]
                    )

        middle = P // 2
        split = middle + VECTOR_GROUPS
        deal(nc.vector.tensor_copy, qb[:, :, :middle, :], q_raw[0][:])
        nc.vector.tensor_copy(ksg[:], ks[:].indirect(offsets[:]))
        nc.vector.tensor_copy(kg[:], kw[:].indirect(offsets[:]))
        deal(nc.vector.tensor_copy, qb[:, :, middle:split, :], q_raw[1][:, :, : PACK * VECTOR_GROUPS])
        deal(nc.scalar.copy, qb[:, :, split:, :], q_raw[1][:, :, PACK * VECTOR_GROUPS :])
        spread_row(pre_row, pre_col, "spread_pre")
        for a, b in ((0, 2), (2, 4)):
            cols = slice(P * a, P * b)
            quantize(qc[:, cols], qsc[:, cols], qb[:, a:b].rearrange("p t m j -> p (t m j)"))
            for t in range(a, b):
                product(score[t][:], qc, qsc, t, kg, ksg)
        spread_row(sg_row, sg_col, "spread_sg")

        for t in range(PACK):
            nc.vector.tensor_reduce(out=nmax[:, t : t + 1], in_=score[t][:], axis=AX.X, op=ALU.max, negate=True)
            nc.scalar.activation(
                out=prob[:, t, :], in_=score[t][:], func=ACT.Exp, bias=nmax[:, t : t + 1], scale=1.0,
                accum_out=rsum[:, t : t + 1],
            )
        for a in (0, 2):
            nc.vector.reciprocal(out=rinv[:, a : a + 2], in_=rsum[:, a : a + 2])
            for t in (a, a + 1):
                nc.vector.tensor_scalar(
                    out=wrow[:, t, :], in0=prob[:, t, :], scalar1=rinv[:, t : t + 1], scalar2=qs_col[:, t : t + 1],
                    op0=ALU.mult, op1=ALU.mult,
                )
        weave(nc.vector.tensor_copy, wb[:], wrow[:])
        quantize(wc[:], wsc[:], wb[:].rearrange("p i t -> p (i t)"))

        deal(nc.scalar.copy, gb[:], g_raw[:])
        c0 = []
        for pair in range(2):
            cols = slice(2 * P * pair, 2 * P * (pair + 1))
            quantize(gc[:, cols], gsc[:, cols], gb[:, 2 * pair : 2 * pair + 2].rearrange("p t m j -> p (t m j)"))
            c0.append(ps.tile([P, 2, I], F32, name=f"c0_{pair}"))
            for s in range(2):
                product(c0[pair][:, s, :], gc, gsc, 2 * pair + s, wc, wsc)

        def gather_and_square(a, b):
            for t in range(a, b):
                nc.vector.tensor_tensor(x[:, t, :], v_raw[t][:].indirect(offsets[:]), pre_row, ALU.mult)
            nc.scalar.activation(out=sq[:, a:b, :], in_=x[:, a:b, :], func=ACT.Square)

        def page_sum(dst, src, a, b):
            nc.vector.tensor_reduce(out=dst[:, a:b, :], in_=pages(src, a, b), axis=AX.X, op=ALU.add)

        def norms(a, b):
            nc.scalar.activation(
                out=rm[:, a:b, :], in_=ssq[:, a:b, :], func=ACT.Abs_reciprocal_sqrt, scale=1.0 / PAGE, bias=EPS
            )
            for t in range(a, b):
                nc.scalar.activation(out=rg[:, t, :], in_=rm[:, t, :], func=ACT.Copy, scale=gain_col[:, t : t + 1])
            nc.scalar.activation(out=r2[:, a:b, :], in_=rm[:, a:b, :], func=ACT.Square, scale=PAGE**-0.5)

        gather_and_square(0, 2)
        page_sum(ssq, sq, 0, 2)
        rm = sb.tile([P, PACK, G], F32, name="rm", tag="graw")
        norms(0, 2)
        gather_and_square(2, 4)

        def mul(out, in0, in1):
            nc.vector.tensor_tensor(out=out, in0=in0, in1=in1, op=ALU.mult)

        mul(cx[:, 0:2, :], c0[0][:], x[:, 0:2, :])
        page_sum(ssq, sq, 2, 4)
        norms(2, 4)
        scale_pages_on_scalar(amp, lambda t: sg_row, rg, 0, 2)
        page_sum(cx_sum, cx, 0, 2)
        mul(cx[:, 2:4, :], c0[1][:], x[:, 2:4, :])
        mul(coef[:, 0:2, :], cx_sum[:, 0:2, :], r2[:, 0:2, :])
        page_sum(cx_sum, cx, 2, 4)
        mul(pages(x_coef, 0, 1), pages(x, 0, 1), per_page(coef, 0, 1))
        mul(coef[:, 2:4, :], cx_sum[:, 2:4, :], r2[:, 2:4, :])
        scale_pages_on_scalar(x_coef, lambda t: x[:, t, :], coef, 2, 4)
        mul(pages(x_coef, 1, 2), pages(x, 1, 2), per_page(coef, 1, 2))
        sg_pages = sg_row.rearrange("p (g j) -> p g j", j=PAGE).unsqueeze(1).to_broadcast([P, 2, G, PAGE])
        mul(pages(amp, 2, 4), sg_pages, per_page(rg, 2, 4))

        for t in (0, 1):
            nc.vector.tensor_tensor(
                out=diff[:, t : t + 1, :], in0=c0[0][:, t : t + 1, :], in1=x_coef[:, t : t + 1, :], op=ALU.subtract
            )
        for t in (0, 1):
            mul(scaled[:, t : t + 1, :], diff[:, t : t + 1, :], amp[:, t : t + 1, :])
        nc.vector.tensor_tensor(out=diff[:, 2:4, :], in0=c0[1][:], in1=x_coef[:, 2:4, :], op=ALU.subtract)
        for t in (0, 1):
            nc.vector.tensor_tensor(
                out=y[:, t : t + 1, :], in0=scaled[:, t : t + 1, :], in1=old_sb[:, t : t + 1, :], op=ALU.add
            )
            nc.sync.dma_start(out=out_rows[:, t : t + 1, :], in_=y[:, t : t + 1, :])
        weave(nc.scalar.copy, yb[:, :, 0:2], y[:, 0:2, :])

        halves = [slice(h * HALF, (h + 1) * HALF) for h in range(2)]
        for cols in halves:
            mul(scaled[:, 2:4, cols], diff[:, 2:4, cols], amp[:, 2:4, cols])
        for cols in halves:
            nc.vector.tensor_tensor(out=y[:, 2:4, cols], in0=scaled[:, 2:4, cols], in1=old_sb[:, 2:4, cols], op=ALU.add)
        nc.sync.dma_start(out=out_rows[:, 2:4, :], in_=y[:, 2:4, :])
        for cols in halves:
            weave(nc.vector.tensor_copy, yb[:, cols, 2:4], y[:, 2:4, cols])
        for cols in halves:
            quantize(yc[:, cols], ysc[:, cols], yb[:, cols, :].rearrange("p i t -> p (i t)"))

        nc.sync.dma_start(out=out_1[0].rearrange("p c r -> p (c r)").bitcast(I32), in_=yc[:].bitcast(I32))
        for quad in range(4):
            queue = nc.scalar if quad % 2 == 0 else nc.sync
            queue.dma_start(
                out=out_2[0, 4 * quad : 4 * quad + 4, :].bitcast(I32),
                in_=ysc[32 * quad : 32 * quad + 4, :].bitcast(I32),
            )
